import numpy as np
import ml_dtypes


def mxq(x, axis, fmt="e4m3"):
    dtype, down = {"e4m3": (ml_dtypes.float8_e4m3fn, 7), "e5m2": (ml_dtypes.float8_e5m2, 14)}[fmt]
    v = np.moveaxis(np.asarray(x, np.float32).astype(ml_dtypes.bfloat16).astype(np.float64), axis, -1)
    blocks = v.reshape(v.shape[:-1] + (-1, 32))
    amax = np.abs(blocks).max(-1, keepdims=True)
    byte = np.maximum(np.where(amax > 0, np.frexp(amax)[1] - 1 + 127, 0) - down, 1)
    scale = np.exp2(byte - 127.0)
    codes = (blocks / scale).astype(np.float32).astype(dtype).astype(np.float64)
    return np.moveaxis((codes * scale).reshape(v.shape), -1, axis)


WIDE = False


def mx_kscale(k):
    if not WIDE:
        return np.ones(k)
    levels = np.array([10, -10, 5, -5, 0])
    if k % 512:
        return np.exp2(np.random.permutation(np.resize(levels, k // 32))).repeat(32)
    a = np.empty((k // 512, 16))
    for p in range(k // 512):
        a[p, :8] = np.random.permutation(np.resize(levels, 8))
        for g in range(8):
            far = levels[np.abs(levels - a[p, g]) >= 10]
            a[p, g + 8] = far[np.random.randint(len(far))]
    return np.exp2(a.ravel()).repeat(32)


def f64(x):
    return np.asarray(x).astype(np.float64)


def striped(idx):
    return np.tile(idx.reshape(-1, 16).T, (8, 1)).astype(np.uint16)


def unstriped(offs):
    return offs[:16].T.reshape(-1).astype(np.int64)


def striped8(idx):
    return np.concatenate([x.reshape(-1, 16).T for x in idx]).astype(np.uint16)


def runs(offs, k):
    lists = np.stack([offs[16 * r : 16 * r + 16].T.reshape(-1) for r in range(8)]).astype(np.int64)
    return lists[np.arange(k) % 512 // 64]


def pack_weight(w):
    k, n = w.shape
    w = f64(np.asarray(w, np.float32).astype(ml_dtypes.bfloat16)).reshape(k // 32, 32, n)
    amax = np.abs(w).max(1)
    byte = np.clip(np.where(amax > 0, np.frexp(amax)[1] - 1 + 127 - 7, 1), 1, 254)
    scaled = (w * np.exp2(127.0 - byte)[:, None, :]).reshape(k, n).astype(np.float32)
    words = np.ascontiguousarray(scaled.reshape(k // 512, 128, 4, n).transpose(0, 1, 3, 2)).astype(ml_dtypes.float8_e4m3fn).view(np.uint8)
    return words, np.ascontiguousarray(byte.astype(np.uint8).reshape(k // 512, 16, n))


def unpack_weight(words, scales):
    g, p, n, _ = words.shape
    vals = np.ascontiguousarray(words).view(ml_dtypes.float8_e4m3fn).astype(np.float64) * np.repeat(np.exp2(scales.astype(np.float64) - 127.0), 8, axis=1)[..., None]
    return vals.transpose(0, 1, 3, 2).reshape(g * 512, n)


K, T, S, G, H, W, U = 512, 1024, 256, 2048, 512, 128, 512


def setup_inputs():
    n = np.random.standard_normal
    s = mx_kscale(K)[:, None]
    packed_xT = pack_weight(n((K, T)) * s)
    packed_dT = pack_weight(n((K, G)) / s)
    perm = np.random.permutation(S)
    perm2 = np.random.permutation(U)
    return {
        "x_words": packed_xT[0],
        "x_scales": packed_xT[1],
        "d_words": packed_dT[0],
        "d_scales": packed_dT[1],
        "gs": (np.random.uniform(0.5, 1.5, (K, 1)) * s).astype(np.float32),
        "offs": striped(np.random.permutation(T)[:S]),
        "ka": striped8(np.random.randint(0, G, (8, H))),
        "kb": striped8(np.random.randint(0, G, (8, H))),
        "n1": striped(perm[:W]),
        "n2": striped(perm[W:]),
        "k1": striped8(np.random.randint(0, G, (8, H))),
        "k2": striped8(np.random.randint(0, G, (8, H))),
        "hz": striped8(np.random.randint(0, T, (8, S))),
        "n3": striped(perm2[:S]),
        "n4": striped(perm2[S:]),
        "n5": striped(np.random.permutation(S)),
        "n6": striped(np.random.permutation(S)),
    }


def reference(x_words, x_scales, d_words, d_scales, gs, offs, ka, kb, n1, n2, k1, k2, hz, n3, n4, n5, n6):
    d_k1 = unpack_weight(d_words, d_scales)[np.arange(K)[:, None], runs(k1, K)]
    d_ka = unpack_weight(d_words, d_scales)[np.arange(K)[:, None], runs(ka, K)]
    xq = unpack_weight(x_words, x_scales)[:, unstriped(offs)]
    d_kb = unpack_weight(d_words, d_scales)[np.arange(K)[:, None], runs(kb, K)]
    h = 0.0625 * (d_ka.T @ xq + d_kb.T @ xq)
    pa = h[:, unstriped(n1)]
    pb = h[:, unstriped(n2)]
    rb = pa - pb
    ra = 0.75 * (pa + pb)
    ua = np.zeros((H, S))
    ua[:, unstriped(n1)] = ra
    ub = ua.copy()
    ub[:, unstriped(n2)] = rb
    z = f64(gs) * ub
    d_k2 = unpack_weight(d_words, d_scales)[np.arange(K)[:, None], runs(k2, K)]
    x_hz = unpack_weight(x_words, x_scales)[np.arange(K)[:, None], runs(hz, K)]
    h2 = 0.0625 * ((d_k1.T @ mxq(z, 0, "e4m3") + d_k2.T @ x_hz))
    st = h2 - h2[:, unstriped(n5)]
    up = np.maximum(st, st[:, unstriped(n6)])
    ph = np.zeros((H, U))
    ph[:, unstriped(n3)] = st
    out = ph.copy()
    out[:, unstriped(n4)] = up
    return out

@@ -1,0 +1,277 @@
+from contextlib import ExitStack
+
+import concourse.mybir as mybir
+
+K, T, S, G, H, W, U = 512, 1024, 256, 2048, 512, 128, 512
+FLOPS = 4 * 2 * K * H * S
+
+F32 = mybir.dt.float32
+BF16 = mybir.dt.bfloat16
+I32 = mybir.dt.int32
+U32 = mybir.dt.uint32
+U16 = mybir.dt.uint16
+U8 = mybir.dt.uint8
+FP8X4 = mybir.dt.float8_e4m3fn_x4
+COPY = mybir.ActivationFunctionType.Copy
+ALU = mybir.AluOpType
+
+P = 128
+HALF = 256
+SPARE = 16
+
+
+def tile_picked_atzmhhaarpagew_none_p_kernel(
+    tc, x_words, x_scales, d_words, d_scales, gs, offs, ka, kb, n1, n2, k1, k2, hz, n3, n4, n5, n6, out
+):
+    nc = tc.nc
+    with ExitStack() as ctx:
+        lists = ctx.enter_context(tc.tile_pool(name="lists", bufs=1))
+        sb = ctx.enter_context(tc.tile_pool(name="sb", bufs=1))
+        psum = ctx.enter_context(tc.psum_pool(name="psum", bufs=1))
+
+        def new(name, shape, dtype, tag=None):
+            return sb.tile(shape, dtype, name=name, tag=tag or name, align_bytes=64)
+
+        def load_list(name, src):
+            tile = lists.tile(list(src.shape), U16, name=name)
+            nc.sync.dma_start(tile[:], src)
+            return tile
+
+        def load_scales(name, src, width):
+            tile = new(name, [P, width], U8)
+            rows = src[0].bitcast(I32).unsqueeze(1).broadcast_to([16, 8, width // 4])
+            nc.sync.dma_start(tile[:].bitcast(I32), rows)
+            return tile
+
+        def load_words(name, src, width):
+            tile = new(name, [P, width], I32)
+            nc.sync.dma_start(tile[:], src[0].rearrange("p n t -> p (n t)").bitcast(I32))
+            return tile
+
+        def half(lst, h):
+            return lst[:, h * HALF // 16 : (h + 1) * HALF // 16]
+
+        def gather_bytes(dst, table, offsets):
+            nc.vector.tensor_copy(dst, table[:].indirect(offsets))
+
+        def gather_words(dst, table, offsets):
+            nc.vector.tensor_copy(dst, table[:].bitcast(U32).indirect(offsets))
+
+        def cleared(name, width):
+            tile = new(name, [P, width], U8)
+            nc.vector.memset(tile[:].bitcast(I32), 0)
+            return tile
+
+        def place_rows(dst, src):
+            for r in range(4):
+                nc.sync.dma_start(dst[r:P:32, :].bitcast(I32), src[8 * r : P : 32, :].bitcast(I32))
+
+        def product(acc, lhs, lhs_scale, rhs, rhs_scale, first):
+            nc.tensor.matmul_mx(
+                out=acc[:, 0:S],
+                lhsT=lhs.bitcast(FP8X4),
+                lhsT_scale=lhs_scale,
+                rhs=rhs.bitcast(FP8X4),
+                rhs_scale=rhs_scale,
+                start=first,
+                stop=not first,
+            )
+
+        x_sc = load_scales("x_sc", x_scales, T)
+        l_offs = load_list("l_offs", offs)
+        d_sc = load_scales("d_sc", d_scales, G)
+        l_ka = load_list("l_ka", ka)
+        l_kb = load_list("l_kb", kb)
+        l_n1 = load_list("l_n1", n1)
+        d_w = load_words("d_w", d_words, G)
+        x_w = load_words("x_w", x_words, T)
+        l_n2 = load_list("l_n2", n2)
+        l_k1 = load_list("l_k1", k1)
+        l_k2 = load_list("l_k2", k2)
+        l_hz = load_list("l_hz", hz)
+        l_n5 = load_list("l_n5", n5)
+        l_n6 = load_list("l_n6", n6)
+        l_n3 = load_list("l_n3", n3)
+        l_n4 = load_list("l_n4", n4)
+
+        placed1 = cleared("placed1", 2 * H + S)
+        placed2 = cleared("placed2", 2 * HALF + S)
+        placed3 = cleared("placed3", 2 * HALF)
+        h2 = [new("h2_%d" % u, [P, S + SPARE], F32) for u in range(4)]
+        st = [new("st_%d" % u, [P, S + SPARE], F32) for u in range(4)]
+        for u in range(4):
+            nc.vector.memset(h2[u][:, S:], 0.0)
+            nc.scalar.activation(st[u][:, S:], h2[u][:, S:], COPY)
+
+        bytes1 = new("bytes1", [P, 2 * H + S], U8, tag="hold_a")
+        gather_bytes(bytes1[:, 2 * H :], x_sc, l_offs[:])
+        gather_bytes(bytes1[:, 0:H], d_sc, l_ka[:])
+        gather_bytes(bytes1[:, H : 2 * H], d_sc, l_kb[:])
+        place_rows(placed1, bytes1)
+        xq_scale = placed1[:, 2 * H :]
+
+        def gather_half(h, tag):
+            words = new("words_h%d" % h, [P, 2, HALF], U32, tag=tag)
+            gather_words(words[:, 0, :], d_w, half(l_ka, h))
+            gather_words(words[:, 1, :], d_w, half(l_kb, h))
+            return words[:].rearrange("p l (m t) -> p l m t", t=4)
+
+        def deal_pair(h, words, tag):
+            dealt = new("dealt_h%d" % h, [P, 2, P], U32, tag=tag)
+            nc.vector.tensor_copy(dealt[:].rearrange("p l (e m) -> p l m e", e=2), words[:, :, :, 0:2])
+            return dealt
+
+        def first_product(b, words_a, words_b, scale_a, scale_b):
+            acc = psum.tile([P, 512], F32, name="acc1_%d" % b)
+            product(acc, words_a, scale_a, xq[:], xq_scale, True)
+            product(acc, words_b, scale_b, xq[:], xq_scale, False)
+            h = new("h_%d" % b, [P, S], F32)
+            if b == 0:
+                nc.scalar.activation(h[:], acc[:, 0:S], COPY, scale=0.0625)
+            else:
+                nc.vector.tensor_scalar_mul(h[:], acc[:, 0:S], 0.0625)
+            return h
+
+        def fetch_pairs(b, h, tag):
+            pa = new("pa_%d" % b, [P, W], F32, tag=tag)
+            pb = new("pb_%d" % b, [P, W], F32)
+            nc.scalar.activation(pa[:], h[:].indirect(l_n1[:]), COPY)
+            nc.scalar.activation(pb[:], h[:].indirect(l_n2[:]), COPY)
+            return pa, pb
+
+        def combine(b, pairs, tag):
+            total = new("total_%d" % b, [P, W], F32, tag=tag)
+            rb = new("rb_%d" % b, [P, W], F32)
+            nc.vector.tensor_tensor(total[:], pairs[0][:], pairs[1][:], ALU.add)
+            nc.vector.tensor_tensor(rb[:], pairs[0][:], pairs[1][:], ALU.subtract)
+            return total, rb
+
+        def put_pairs(b, both, other):
+            ubs = [new("ub_%d" % i, [P, S], F32) for i in (b, b + 1)]
+            for ub, (total, rb) in zip(ubs, (both, other)):
+                nc.scalar.activation(ub[:].indirect(l_n1[:]), total[:], COPY, scale=0.75)
+            for ub, (total, rb) in zip(ubs, (both, other)):
+                nc.scalar.activation(ub[:].indirect(l_n2[:]), rb[:], COPY)
+            return ubs
+
+        plane0 = new("plane0", [P, S], F32)
+        plane1 = new("plane1", [P, S], F32, tag="hold_z")
+
+        def move_planes(h, ub):
+            nc.sync.dma_start(plane0[64 * h : 64 * h + 64, :], ub[0:64, :])
+            nc.sync.dma_start(plane1[64 * h : 64 * h + 64, :], ub[64:128, :])
+
+        words0 = gather_half(0, None)
+        xq = new("xq", [P, S], U32)
+        gather_words(xq[:], x_w, l_offs[:])
+        dealt0 = deal_pair(0, words0, "hold_g")
+        scale_ab = new("scale_ab", [P, 4, 2, 64], U8)
+        nc.vector.tensor_copy(
+            scale_ab[:], placed1[:, 0 : 2 * H].rearrange("p (g m t) -> p g t m", m=64, t=4)[:, :, 0:2, :]
+        )
+        scale_ab = scale_ab[:].rearrange("p g e m -> p g (e m)")
+        h_a = first_product(0, dealt0[:, 0, :], dealt0[:, 1, :], scale_ab[:, 0, :], scale_ab[:, 2, :])
+        pairs_a = fetch_pairs(0, h_a, None)
+        gains = new("gains", [P, 4], F32, tag="hold_g")
+        nc.sync.dma_start(gains[:], gs.rearrange("(p t) o -> p (t o)", t=4))
+
+        words1 = gather_half(1, "hold_a")
+        dealt1 = deal_pair(1, words1, None)
+        dealt_cd = new("dealt_cd", [P, 2, 2, P], U32, tag="hold_cd")
+        for h, words in enumerate((words0, words1)):
+            nc.vector.tensor_copy(
+                dealt_cd[:, :, :, 64 * h : 64 * h + 64].rearrange("p l t m -> p l m t"), words[:, :, :, 2:4]
+            )
+        scale_cd = new("scale_cd", [P, 2, 2, P], U8, tag="hold_s")
+        nc.vector.tensor_copy(
+            scale_cd[:], placed1[:, 0 : 2 * H].rearrange("p (l m t) -> p l t m", l=2, t=4)[:, :, 2:4, :]
+        )
+        h_b = first_product(1, dealt1[:, 0, :], dealt1[:, 1, :], scale_ab[:, 1, :], scale_ab[:, 3, :])
+        pairs_b = fetch_pairs(1, h_b, None)
+        both_a = combine(0, pairs_a, None)
+        h_c = first_product(2, dealt_cd[:, 0, 0, :], dealt_cd[:, 1, 0, :], scale_cd[:, 0, 0, :], scale_cd[:, 1, 0, :])
+        both_b = combine(1, pairs_b, None)
+        h_d = first_product(3, dealt_cd[:, 0, 1, :], dealt_cd[:, 1, 1, :], scale_cd[:, 0, 1, :], scale_cd[:, 1, 1, :])
+        ub_a, ub_b = put_pairs(0, both_a, both_b)
+        pairs_c = fetch_pairs(2, h_c, None)
+        pairs_d = fetch_pairs(3, h_d, None)
+
+        bytes2 = new("bytes2", [P, 2 * HALF + S], U8, tag="hold_cd")
+        gather_bytes(bytes2[:, 0:HALF], d_sc, half(l_k1, 0))
+        gather_bytes(bytes2[:, HALF : 2 * HALF], d_sc, half(l_k2, 0))
+        gather_bytes(bytes2[:, 2 * HALF :], x_sc, l_hz[:])
+        move_planes(0, ub_a)
+        move_planes(1, ub_b)
+        place_rows(placed2, bytes2)
+        words2 = new("words2", [P, 3, HALF], U32, tag="hold_s")
+        gather_words(words2[:, 1, :], d_w, half(l_k2, 0))
+        gather_words(words2[:, 2, :], x_w, l_hz[:])
+        both_c = combine(2, pairs_c, None)
+        gather_words(words2[:, 0, :], d_w, half(l_k1, 0))
+        both_d = combine(3, pairs_d, None)
+        xh, xh_scale = words2[:, 2, :], placed2[:, 2 * HALF :]
+        ub_c, ub_d = put_pairs(2, both_c, both_d)
+
+        z = new("z", [P, S, 4], BF16)
+        for t, plane in enumerate((plane0, plane1)):
+            nc.vector.tensor_scalar_mul(z[:, :, t], plane[:], gains[:, t : t + 1])
+        last_gains = new("last_gains", [P, 2], F32, tag="hold_z")
+        nc.vector.tensor_copy(last_gains[:], gains[:, 2:4])
+        for t, plane in enumerate((ub_c, ub_d)):
+            nc.vector.tensor_scalar_mul(z[:, :, 2 + t], plane[:], last_gains[:, t : t + 1])
+        z_words = new("z_words", [P, S], U32)
+        z_scale = new("z_scale", [P, S], U8)
+        nc.vector.quantize_mx(out=z_words[:].bitcast(FP8X4), scales=z_scale[:], in_=z[:].rearrange("p n t -> p (n t)"))
+
+
+        def second_product(u, words, placed):
+            cols = slice(P * (u % 2), P * (u % 2) + P)
+            acc = psum.tile([P, 512], F32, name="acc2_%d" % u)
+            product(acc, words[:, 1, cols], placed[:, HALF : 2 * HALF][:, cols], xh, xh_scale, True)
+            product(acc, words[:, 0, cols], placed[:, 0:HALF][:, cols], z_words[:], z_scale[:], False)
+            if u == 0:
+                nc.scalar.activation(h2[u][:, 0:S], acc[:, 0:S], COPY, scale=0.0625)
+            else:
+                nc.vector.tensor_scalar_mul(h2[u][:, 0:S], acc[:, 0:S], 0.0625)
+
+        def step(u):
+            other = new("other_%d" % u, [P, S], F32, tag="hold_d" if u == 0 else None)
+            nc.scalar.activation(other[:], h2[u][:].indirect(l_n5[:]), COPY)
+            nc.vector.tensor_tensor(st[u][:, 0:S], h2[u][:, 0:S], other[:], ALU.subtract)
+
+        def rival_and_first_put(u):
+            rival = new("rival_%d" % u, [P, S], F32, tag="hold_e" if u == 0 else None)
+            up = new("up_%d" % u, [P, S], F32)
+            page = new("page_%d" % u, [P, U], F32)
+            nc.scalar.activation(rival[:], st[u][:].indirect(l_n6[:]), COPY)
+            nc.vector.tensor_tensor(up[:], st[u][:, 0:S], rival[:], ALU.max)
+            nc.scalar.activation(page[:].indirect(l_n3[:]), st[u][:, 0:S], COPY)
+            return up, page
+
+        def second_put(u, up, page):
+            nc.scalar.activation(page[:].indirect(l_n4[:]), up[:], COPY)
+            nc.sync.dma_start(out[P * u : P * u + P, :], page[:])
+
+        second_product(0, words2, placed2)
+        second_product(1, words2, placed2)
+        step(0)
+        bytes3 = new("bytes3", [P, 2 * HALF], U8, tag="hold_d")
+        gather_bytes(bytes3[:, 0:HALF], d_sc, half(l_k1, 1))
+        gather_bytes(bytes3[:, HALF:], d_sc, half(l_k2, 1))
+        place_rows(placed3, bytes3)
+        step(1)
+        first = rival_and_first_put(0)
+        words3 = new("words3", [P, 2, HALF], U32, tag="hold_e")
+        gather_words(words3[:, 1, :], d_w, half(l_k2, 1))
+        gather_words(words3[:, 0, :], d_w, half(l_k1, 1))
+        second = rival_and_first_put(1)
+        second_put(0, *first)
+        second_put(1, *second)
+        for u in (2, 3):
+            second_product(u, words3, placed3)
+        for u in (2, 3):
+            step(u)
+        first = rival_and_first_put(2)
+        second = rival_and_first_put(3)
+        second_put(2, *first)
+        second_put(3, *second)

@@ -66,15 +66,15 @@ def tile_picked_atzmhhaarpagew_none_p_kernel(
             for r in range(4):
                 nc.sync.dma_start(dst[r:P:32, :].bitcast(I32), src[8 * r : P : 32, :].bitcast(I32))
 
-        def product(acc, lhs, lhs_scale, rhs, rhs_scale, first):
+        def product(acc, lhs, lhs_scale, rhs, rhs_scale, start, stop):
             nc.tensor.matmul_mx(
-                out=acc[:, 0:S],
+                out=acc,
                 lhsT=lhs.bitcast(FP8X4),
                 lhsT_scale=lhs_scale,
                 rhs=rhs.bitcast(FP8X4),
                 rhs_scale=rhs_scale,
-                start=first,
-                stop=not first,
+                start=start,
+                stop=stop,
             )
 
         x_sc = load_scales("x_sc", x_scales, T)
@@ -83,13 +83,13 @@ def tile_picked_atzmhhaarpagew_none_p_kernel(
         l_ka = load_list("l_ka", ka)
         l_kb = load_list("l_kb", kb)
         l_n1 = load_list("l_n1", n1)
-        d_w = load_words("d_w", d_words, G)
-        x_w = load_words("x_w", x_words, T)
         l_n2 = load_list("l_n2", n2)
+        d_w = load_words("d_w", d_words, G)
         l_k1 = load_list("l_k1", k1)
         l_k2 = load_list("l_k2", k2)
         l_hz = load_list("l_hz", hz)
         l_n5 = load_list("l_n5", n5)
+        x_w = load_words("x_w", x_words, T)
         l_n6 = load_list("l_n6", n6)
         l_n3 = load_list("l_n3", n3)
         l_n4 = load_list("l_n4", n4)
@@ -110,21 +110,10 @@ def tile_picked_atzmhhaarpagew_none_p_kernel(
         place_rows(placed1, bytes1)
         xq_scale = placed1[:, 2 * H :]
 
-        def gather_half(h, tag):
-            words = new("words_h%d" % h, [P, 2, HALF], U32, tag=tag)
-            gather_words(words[:, 0, :], d_w, half(l_ka, h))
-            gather_words(words[:, 1, :], d_w, half(l_kb, h))
-            return words[:].rearrange("p l (m t) -> p l m t", t=4)
-
-        def deal_pair(h, words, tag):
-            dealt = new("dealt_h%d" % h, [P, 2, P], U32, tag=tag)
-            nc.vector.tensor_copy(dealt[:].rearrange("p l (e m) -> p l m e", e=2), words[:, :, :, 0:2])
-            return dealt
-
         def first_product(b, words_a, words_b, scale_a, scale_b):
             acc = psum.tile([P, 512], F32, name="acc1_%d" % b)
-            product(acc, words_a, scale_a, xq[:], xq_scale, True)
-            product(acc, words_b, scale_b, xq[:], xq_scale, False)
+            product(acc[:, 0:S], words_a, scale_a, xq[:], xq_scale, True, False)
+            product(acc[:, 0:S], words_b, scale_b, xq[:], xq_scale, False, True)
             h = new("h_%d" % b, [P, S], F32)
             if b == 0:
                 nc.scalar.activation(h[:], acc[:, 0:S], COPY, scale=0.0625)
@@ -132,27 +121,18 @@ def tile_picked_atzmhhaarpagew_none_p_kernel(
                 nc.vector.tensor_scalar_mul(h[:], acc[:, 0:S], 0.0625)
             return h
 
-        def fetch_pairs(b, h, tag):
-            pa = new("pa_%d" % b, [P, W], F32, tag=tag)
-            pb = new("pb_%d" % b, [P, W], F32)
-            nc.scalar.activation(pa[:], h[:].indirect(l_n1[:]), COPY)
-            nc.scalar.activation(pb[:], h[:].indirect(l_n2[:]), COPY)
-            return pa, pb
-
         def combine(b, pairs, tag):
             total = new("total_%d" % b, [P, W], F32, tag=tag)
             rb = new("rb_%d" % b, [P, W], F32)
-            nc.vector.tensor_tensor(total[:], pairs[0][:], pairs[1][:], ALU.add)
-            nc.vector.tensor_tensor(rb[:], pairs[0][:], pairs[1][:], ALU.subtract)
+            nc.vector.tensor_tensor(total[:], pairs[0], pairs[1], ALU.add)
+            nc.vector.tensor_tensor(rb[:], pairs[0], pairs[1], ALU.subtract)
             return total, rb
 
-        def put_pairs(b, both, other):
-            ubs = [new("ub_%d" % i, [P, S], F32) for i in (b, b + 1)]
-            for ub, (total, rb) in zip(ubs, (both, other)):
-                nc.scalar.activation(ub[:].indirect(l_n1[:]), total[:], COPY, scale=0.75)
-            for ub, (total, rb) in zip(ubs, (both, other)):
-                nc.scalar.activation(ub[:].indirect(l_n2[:]), rb[:], COPY)
-            return ubs
+        def fetch(pairs, h, side):
+            nc.scalar.activation(pairs[side], h[:].indirect((l_n1, l_n2)[side][:]), COPY)
+
+        def put(ub, both, side):
+            nc.scalar.activation(ub[:].indirect((l_n1, l_n2)[side][:]), both[side][:], COPY, scale=(0.75, 1.0)[side])
 
         plane0 = new("plane0", [P, S], F32)
         plane1 = new("plane1", [P, S], F32, tag="hold_z")
@@ -161,78 +141,123 @@ def tile_picked_atzmhhaarpagew_none_p_kernel(
             nc.sync.dma_start(plane0[64 * h : 64 * h + 64, :], ub[0:64, :])
             nc.sync.dma_start(plane1[64 * h : 64 * h + 64, :], ub[64:128, :])
 
-        words0 = gather_half(0, None)
+        placed_halves = placed1[:, 0 : 2 * H].rearrange("p (l h m t) -> p h l t m", l=2, h=2, t=4)
+        placed_whole = placed1[:, 0 : 2 * H].rearrange("p (l m t) -> p t l m", l=2, t=4)
+
+        def deal_scales(h):
+            dealt = new("scale_h%d" % h, [P, 2, 2, 64], U8, tag="hold_cd" if h == 0 else None)
+            nc.vector.tensor_copy(dealt[:], placed_halves[:, h, :, 0:2, :])
+            return dealt[:].rearrange("p l e m -> p l (e m)")
+
+        ub = [new("ub_%d" % b, [P, S], F32) for b in range(4)]
+        early = new("early", [P, 3, HALF], U32)
+        gather_words(early[:, 0, :], d_w, half(l_ka, 0))
+        gather_words(early[:, 2, :], d_w, half(l_kb, 0))
+        gather_words(early[:, 1, :], d_w, half(l_ka, 1))
         xq = new("xq", [P, S], U32)
         gather_words(xq[:], x_w, l_offs[:])
-        dealt0 = deal_pair(0, words0, "hold_g")
-        scale_ab = new("scale_ab", [P, 4, 2, 64], U8)
-        nc.vector.tensor_copy(
-            scale_ab[:], placed1[:, 0 : 2 * H].rearrange("p (g m t) -> p g t m", m=64, t=4)[:, :, 0:2, :]
-        )
-        scale_ab = scale_ab[:].rearrange("p g e m -> p g (e m)")
-        h_a = first_product(0, dealt0[:, 0, :], dealt0[:, 1, :], scale_ab[:, 0, :], scale_ab[:, 2, :])
-        pairs_a = fetch_pairs(0, h_a, None)
+        early_rows = early[:].rearrange("p g (m t) -> p g m t", t=4)
+        low_early = new("low_early", [P, 3, P], U32)
+        nc.vector.tensor_copy(low_early[:].rearrange("p g (e m) -> p g m e", e=2), early_rows[:, :, :, 0:2])
+        scale_a = deal_scales(0)
+        h_a = first_product(0, low_early[:, 0, :], low_early[:, 2, :], scale_a[:, 0, :], scale_a[:, 1, :])
+        pairs_ab = new("pairs_ab", [P, 4, W], F32)
+        pairs_a = [pairs_ab[:, 0, :], pairs_ab[:, 1, :]]
+        pairs_b = [pairs_ab[:, 2, :], pairs_ab[:, 3, :]]
+        fetch(pairs_a, h_a, 0)
+        fetch(pairs_a, h_a, 1)
+
+        last = new("last", [P, HALF], U32, tag="hold_a")
+        gather_words(last[:], d_w, half(l_kb, 1))
+        last_rows = last[:].rearrange("p (m t) -> p m t", t=4)
+        low_last = new("low_last", [P, P], U32, tag="hold_g")
+        nc.vector.tensor_copy(low_last[:].rearrange("p (e m) -> p m e", e=2), last_rows[:, :, 0:2])
+        scale_b = deal_scales(1)
+        high = new("high", [P, 2, 4, 64], U32, tag="hold_cd")
+        nc.vector.tensor_copy(high[:, :, 3, :].rearrange("p t m -> p m t"), last_rows[:, :, 2:4])
+        nc.vector.tensor_copy(high[:, :, 0:3, :].rearrange("p t g m -> p g m t"), early_rows[:, :, :, 2:4])
+        high = high[:].rearrange("p t (l h) m -> p t l (h m)", l=2)
+        scale_cd = new("scale_cd", [P, 2, 2, P], U8, tag="hold_s")
+        scale_c, scale_d = scale_cd[:, 0], scale_cd[:, 1]
+        nc.vector.tensor_copy(scale_c, placed_whole[:, 2])
+        h_b = first_product(1, low_early[:, 1, :], low_last[:], scale_b[:, 0, :], scale_b[:, 1, :])
         gains = new("gains", [P, 4], F32, tag="hold_g")
         nc.sync.dma_start(gains[:], gs.rearrange("(p t) o -> p (t o)", t=4))
-
-        words1 = gather_half(1, "hold_a")
-        dealt1 = deal_pair(1, words1, None)
-        dealt_cd = new("dealt_cd", [P, 2, 2, P], U32, tag="hold_cd")
-        for h, words in enumerate((words0, words1)):
-            nc.vector.tensor_copy(
-                dealt_cd[:, :, :, 64 * h : 64 * h + 64].rearrange("p l t m -> p l m t"), words[:, :, :, 2:4]
-            )
-        scale_cd = new("scale_cd", [P, 2, 2, P], U8, tag="hold_s")
-        nc.vector.tensor_copy(
-            scale_cd[:], placed1[:, 0 : 2 * H].rearrange("p (l m t) -> p l t m", l=2, t=4)[:, :, 2:4, :]
-        )
-        h_b = first_product(1, dealt1[:, 0, :], dealt1[:, 1, :], scale_ab[:, 1, :], scale_ab[:, 3, :])
-        pairs_b = fetch_pairs(1, h_b, None)
+        fetch(pairs_b, h_b, 0)
+        fetch(pairs_b, h_b, 1)
         both_a = combine(0, pairs_a, None)
-        h_c = first_product(2, dealt_cd[:, 0, 0, :], dealt_cd[:, 1, 0, :], scale_cd[:, 0, 0, :], scale_cd[:, 1, 0, :])
-        both_b = combine(1, pairs_b, None)
-        h_d = first_product(3, dealt_cd[:, 0, 1, :], dealt_cd[:, 1, 1, :], scale_cd[:, 0, 1, :], scale_cd[:, 1, 1, :])
-        ub_a, ub_b = put_pairs(0, both_a, both_b)
-        pairs_c = fetch_pairs(2, h_c, None)
-        pairs_d = fetch_pairs(3, h_d, None)
+        nc.vector.tensor_copy(scale_d, placed_whole[:, 3])
+        h_c = first_product(2, high[:, 0, 0, :], high[:, 0, 1, :], scale_c[:, 0, :], scale_c[:, 1, :])
+        both_b = combine(1, pairs_b, "hold_b")
+        h_d = first_product(3, high[:, 1, 0, :], high[:, 1, 1, :], scale_d[:, 0, :], scale_d[:, 1, :])
+        for side in range(2):
+            put(ub[0], both_a, side)
+            put(ub[1], both_b, side)
+        move_planes(0, ub[0])
+        move_planes(1, ub[1])
+        pairs_cd = new("pairs_cd", [P, 4, W], F32, tag="hold_b")
+        pairs_c = [pairs_cd[:, 0, :], pairs_cd[:, 1, :]]
+        pairs_d = [pairs_cd[:, 2, :], pairs_cd[:, 3, :]]
+        for pairs, h in ((pairs_c, h_c), (pairs_d, h_d)):
+            fetch(pairs, h, 0)
+            fetch(pairs, h, 1)
 
         bytes2 = new("bytes2", [P, 2 * HALF + S], U8, tag="hold_cd")
         gather_bytes(bytes2[:, 0:HALF], d_sc, half(l_k1, 0))
         gather_bytes(bytes2[:, HALF : 2 * HALF], d_sc, half(l_k2, 0))
         gather_bytes(bytes2[:, 2 * HALF :], x_sc, l_hz[:])
-        move_planes(0, ub_a)
-        move_planes(1, ub_b)
         place_rows(placed2, bytes2)
         words2 = new("words2", [P, 3, HALF], U32, tag="hold_s")
         gather_words(words2[:, 1, :], d_w, half(l_k2, 0))
         gather_words(words2[:, 2, :], x_w, l_hz[:])
         both_c = combine(2, pairs_c, None)
-        gather_words(words2[:, 0, :], d_w, half(l_k1, 0))
         both_d = combine(3, pairs_d, None)
+        gather_words(words2[:, 0, :], d_w, half(l_k1, 0))
         xh, xh_scale = words2[:, 2, :], placed2[:, 2 * HALF :]
-        ub_c, ub_d = put_pairs(2, both_c, both_d)
+        words2 = (words2[:, 0, :], words2[:, 1, :])
+        for side in range(2):
+            put(ub[2], both_c, side)
+            put(ub[3], both_d, side)
+        ub_c, ub_d = ub[2], ub[3]
 
-        z = new("z", [P, S, 4], BF16)
-        for t, plane in enumerate((plane0, plane1)):
-            nc.vector.tensor_scalar_mul(z[:, :, t], plane[:], gains[:, t : t + 1])
+        halves = (slice(0, P), slice(P, S))
+        z = [new("z_%d" % c, [P, P, 4], BF16) for c in range(2)]
+
+        def weave(t, plane, gain):
+            for c in range(2):
+                nc.vector.tensor_scalar_mul(z[c][:, :, t], plane[:, halves[c]], gain)
+
+        weave(0, plane0, gains[:, 0:1])
+        weave(1, plane1, gains[:, 1:2])
         last_gains = new("last_gains", [P, 2], F32, tag="hold_z")
         nc.vector.tensor_copy(last_gains[:], gains[:, 2:4])
-        for t, plane in enumerate((ub_c, ub_d)):
-            nc.vector.tensor_scalar_mul(z[:, :, 2 + t], plane[:], last_gains[:, t : t + 1])
+        weave(2, ub_c, last_gains[:, 0:1])
+        weave(3, ub_d, last_gains[:, 1:2])
         z_words = new("z_words", [P, S], U32)
         z_scale = new("z_scale", [P, S], U8)
-        nc.vector.quantize_mx(out=z_words[:].bitcast(FP8X4), scales=z_scale[:], in_=z[:].rearrange("p n t -> p (n t)"))
-
+        for c in range(2):
+            nc.vector.quantize_mx(
+                out=z_words[:, halves[c]].bitcast(FP8X4),
+                scales=z_scale[:, halves[c]],
+                in_=z[c][:].rearrange("p n t -> p (n t)"),
+            )
 
         def second_product(u, words, placed):
             cols = slice(P * (u % 2), P * (u % 2) + P)
             acc = psum.tile([P, 512], F32, name="acc2_%d" % u)
-            product(acc, words[:, 1, cols], placed[:, HALF : 2 * HALF][:, cols], xh, xh_scale, True)
-            product(acc, words[:, 0, cols], placed[:, 0:HALF][:, cols], z_words[:], z_scale[:], False)
-            if u == 0:
-                nc.scalar.activation(h2[u][:, 0:S], acc[:, 0:S], COPY, scale=0.0625)
-            else:
-                nc.vector.tensor_scalar_mul(h2[u][:, 0:S], acc[:, 0:S], 0.0625)
+            product(acc[:, 0:S], words[1][:, cols], placed[:, HALF : 2 * HALF][:, cols], xh, xh_scale, True, False)
+            pieces = halves if u == 0 else (slice(0, S),)
+            for piece in pieces:
+                product(
+                    acc[:, piece],
+                    words[0][:, cols],
+                    placed[:, 0:HALF][:, cols],
+                    z_words[:, piece],
+                    z_scale[:, piece],
+                    False,
+                    piece.stop == S,
+                )
+            nc.vector.tensor_scalar_mul(h2[u][:, 0:S], acc[:, 0:S], 0.0625)
 
         def step(u):
             other = new("other_%d" % u, [P, S], F32, tag="hold_d" if u == 0 else None)
@@ -268,7 +293,7 @@ def tile_picked_atzmhhaarpagew_none_p_kernel(
         second_put(0, *first)
         second_put(1, *second)
         for u in (2, 3):
-            second_product(u, words3, placed3)
+            second_product(u, (words3[:, 0, :], words3[:, 1, :]), placed3)
         for u in (2, 3):
             step(u)
         first = rival_and_first_put(2)

@@ -134,75 +134,50 @@ def tile_picked_atzmhhaarpagew_none_p_kernel(
         def put(ub, both, side):
             nc.scalar.activation(ub[:].indirect((l_n1, l_n2)[side][:]), both[side][:], COPY, scale=(0.75, 1.0)[side])
 
-        plane0 = new("plane0", [P, S], F32)
-        plane1 = new("plane1", [P, S], F32, tag="hold_z")
-
-        def move_planes(h, ub):
-            nc.sync.dma_start(plane0[64 * h : 64 * h + 64, :], ub[0:64, :])
-            nc.sync.dma_start(plane1[64 * h : 64 * h + 64, :], ub[64:128, :])
-
-        placed_halves = placed1[:, 0 : 2 * H].rearrange("p (l h m t) -> p h l t m", l=2, h=2, t=4)
-        placed_whole = placed1[:, 0 : 2 * H].rearrange("p (l m t) -> p t l m", l=2, t=4)
-
-        def deal_scales(h):
-            dealt = new("scale_h%d" % h, [P, 2, 2, 64], U8, tag="hold_cd" if h == 0 else None)
-            nc.vector.tensor_copy(dealt[:], placed_halves[:, h, :, 0:2, :])
-            return dealt[:].rearrange("p l e m -> p l (e m)")
-
-        ub = [new("ub_%d" % b, [P, S], F32) for b in range(4)]
-        early = new("early", [P, 3, HALF], U32)
-        gather_words(early[:, 0, :], d_w, half(l_ka, 0))
-        gather_words(early[:, 2, :], d_w, half(l_kb, 0))
-        gather_words(early[:, 1, :], d_w, half(l_ka, 1))
+        placed_rows = placed1[:, 0 : 2 * H].rearrange("p (l m t) -> p t l m", l=2, t=4)
+        words1 = new("words1", [P, 2, H], U32)
+        gather_words(words1[:, 0, :], d_w, l_ka[:])
+        gather_words(words1[:, 1, :], d_w, l_kb[:])
+        word_rows = words1[:].rearrange("p l (m t) -> p l m t", t=4)
         xq = new("xq", [P, S], U32)
         gather_words(xq[:], x_w, l_offs[:])
-        early_rows = early[:].rearrange("p g (m t) -> p g m t", t=4)
-        low_early = new("low_early", [P, 3, P], U32)
-        nc.vector.tensor_copy(low_early[:].rearrange("p g (e m) -> p g m e", e=2), early_rows[:, :, :, 0:2])
-        scale_a = deal_scales(0)
-        h_a = first_product(0, low_early[:, 0, :], low_early[:, 2, :], scale_a[:, 0, :], scale_a[:, 1, :])
-        pairs_ab = new("pairs_ab", [P, 4, W], F32)
-        pairs_a = [pairs_ab[:, 0, :], pairs_ab[:, 1, :]]
-        pairs_b = [pairs_ab[:, 2, :], pairs_ab[:, 3, :]]
-        fetch(pairs_a, h_a, 0)
-        fetch(pairs_a, h_a, 1)
-
-        last = new("last", [P, HALF], U32, tag="hold_a")
-        gather_words(last[:], d_w, half(l_kb, 1))
-        last_rows = last[:].rearrange("p (m t) -> p m t", t=4)
-        low_last = new("low_last", [P, P], U32, tag="hold_g")
-        nc.vector.tensor_copy(low_last[:].rearrange("p (e m) -> p m e", e=2), last_rows[:, :, 0:2])
-        scale_b = deal_scales(1)
-        high = new("high", [P, 2, 4, 64], U32, tag="hold_cd")
-        nc.vector.tensor_copy(high[:, :, 3, :].rearrange("p t m -> p m t"), last_rows[:, :, 2:4])
-        nc.vector.tensor_copy(high[:, :, 0:3, :].rearrange("p t g m -> p g m t"), early_rows[:, :, :, 2:4])
-        high = high[:].rearrange("p t (l h) m -> p t l (h m)", l=2)
-        scale_cd = new("scale_cd", [P, 2, 2, P], U8, tag="hold_s")
-        scale_c, scale_d = scale_cd[:, 0], scale_cd[:, 1]
-        nc.vector.tensor_copy(scale_c, placed_whole[:, 2])
-        h_b = first_product(1, low_early[:, 1, :], low_last[:], scale_b[:, 0, :], scale_b[:, 1, :])
+        first_words = new("first_words", [P, 2, P], U32, tag="hold_g")
+        nc.vector.tensor_copy(first_words[:], word_rows[:, :, :, 0])
+        first_scales = new("first_scales", [P, 2, P], U8)
+        nc.vector.tensor_copy(first_scales[:], placed_rows[:, 0])
+        h = [first_product(0, first_words[:, 0, :], first_words[:, 1, :], first_scales[:, 0, :], first_scales[:, 1, :])]
         gains = new("gains", [P, 4], F32, tag="hold_g")
         nc.sync.dma_start(gains[:], gs.rearrange("(p t) o -> p (t o)", t=4))
-        fetch(pairs_b, h_b, 0)
-        fetch(pairs_b, h_b, 1)
-        both_a = combine(0, pairs_a, None)
-        nc.vector.tensor_copy(scale_d, placed_whole[:, 3])
-        h_c = first_product(2, high[:, 0, 0, :], high[:, 0, 1, :], scale_c[:, 0, :], scale_c[:, 1, :])
-        both_b = combine(1, pairs_b, "hold_b")
-        h_d = first_product(3, high[:, 1, 0, :], high[:, 1, 1, :], scale_d[:, 0, :], scale_d[:, 1, :])
+
+        rest_words = new("rest_words", [P, 3, 2, P], U32, tag="hold_a")
+        nc.vector.tensor_copy(rest_words[:].rearrange("p t l m -> p l m t"), word_rows[:, :, :, 1:4])
+        rest_scales = new("rest_scales", [P, 3, 2, P], U8, tag="hold_s")
+        nc.vector.tensor_copy(rest_scales[:, 0], placed_rows[:, 1])
+        nc.vector.tensor_copy(rest_scales[:, 1:3], placed_rows[:, 2:4])
+
+        def rest_product(t):
+            words, scales = rest_words[:, t - 1], rest_scales[:, t - 1]
+            return first_product(t, words[:, 0, :], words[:, 1, :], scales[:, 0, :], scales[:, 1, :])
+
+        ub = [new("ub_%d" % t, [P, S], F32) for t in range(4)]
+        pair_tiles = [new("pairs_%d" % t, [P, 2, W], F32) for t in range(4)]
+        pairs = [[tile[:, 0, :], tile[:, 1, :]] for tile in pair_tiles]
+        h.append(rest_product(1))
+        for t in (0, 1):
+            fetch(pairs[t], h[t], 0)
+            fetch(pairs[t], h[t], 1)
+        h.append(rest_product(2))
+        both_a = combine(0, pairs[0], None)
+        h.append(rest_product(3))
+        both_b = combine(1, pairs[1], None)
         for side in range(2):
             put(ub[0], both_a, side)
             put(ub[1], both_b, side)
-        move_planes(0, ub[0])
-        move_planes(1, ub[1])
-        pairs_cd = new("pairs_cd", [P, 4, W], F32, tag="hold_b")
-        pairs_c = [pairs_cd[:, 0, :], pairs_cd[:, 1, :]]
-        pairs_d = [pairs_cd[:, 2, :], pairs_cd[:, 3, :]]
-        for pairs, h in ((pairs_c, h_c), (pairs_d, h_d)):
-            fetch(pairs, h, 0)
-            fetch(pairs, h, 1)
+        for t in (2, 3):
+            fetch(pairs[t], h[t], 0)
+            fetch(pairs[t], h[t], 1)
 
-        bytes2 = new("bytes2", [P, 2 * HALF + S], U8, tag="hold_cd")
+        bytes2 = new("bytes2", [P, 2 * HALF + S], U8, tag="hold_a")
         gather_bytes(bytes2[:, 0:HALF], d_sc, half(l_k1, 0))
         gather_bytes(bytes2[:, HALF : 2 * HALF], d_sc, half(l_k2, 0))
         gather_bytes(bytes2[:, 2 * HALF :], x_sc, l_hz[:])
@@ -210,15 +185,14 @@ def tile_picked_atzmhhaarpagew_none_p_kernel(
         words2 = new("words2", [P, 3, HALF], U32, tag="hold_s")
         gather_words(words2[:, 1, :], d_w, half(l_k2, 0))
         gather_words(words2[:, 2, :], x_w, l_hz[:])
-        both_c = combine(2, pairs_c, None)
-        both_d = combine(3, pairs_d, None)
+        both_c = combine(2, pairs[2], None)
+        both_d = combine(3, pairs[3], None)
         gather_words(words2[:, 0, :], d_w, half(l_k1, 0))
         xh, xh_scale = words2[:, 2, :], placed2[:, 2 * HALF :]
         words2 = (words2[:, 0, :], words2[:, 1, :])
         for side in range(2):
             put(ub[2], both_c, side)
             put(ub[3], both_d, side)
-        ub_c, ub_d = ub[2], ub[3]
 
         halves = (slice(0, P), slice(P, S))
         z = [new("z_%d" % c, [P, P, 4], BF16) for c in range(2)]
@@ -227,12 +201,8 @@ def tile_picked_atzmhhaarpagew_none_p_kernel(
             for c in range(2):
                 nc.vector.tensor_scalar_mul(z[c][:, :, t], plane[:, halves[c]], gain)
 
-        weave(0, plane0, gains[:, 0:1])
-        weave(1, plane1, gains[:, 1:2])
-        last_gains = new("last_gains", [P, 2], F32, tag="hold_z")
-        nc.vector.tensor_copy(last_gains[:], gains[:, 2:4])
-        weave(2, ub_c, last_gains[:, 0:1])
-        weave(3, ub_d, last_gains[:, 1:2])
+        for t in range(4):
+            weave(t, ub[t], gains[:, t : t + 1])
         z_words = new("z_words", [P, S], U32)
         z_scale = new("z_scale", [P, S], U8)
         for c in range(2):

@@ -16,8 +16,10 @@ COPY = mybir.ActivationFunctionType.Copy
 ALU = mybir.AluOpType
 
 P = 128
-HALF = 256
+BANK = 512
+HALF = H // 2
 SPARE = 16
+SIXTEENTH = 0.0625
 
 
 def tile_picked_atzmhhaarpagew_none_p_kernel(
@@ -26,11 +28,11 @@ def tile_picked_atzmhhaarpagew_none_p_kernel(
     nc = tc.nc
     with ExitStack() as ctx:
         lists = ctx.enter_context(tc.tile_pool(name="lists", bufs=1))
-        sb = ctx.enter_context(tc.tile_pool(name="sb", bufs=1))
+        sbuf = ctx.enter_context(tc.tile_pool(name="sbuf", bufs=1))
         psum = ctx.enter_context(tc.psum_pool(name="psum", bufs=1))
 
         def new(name, shape, dtype, tag=None):
-            return sb.tile(shape, dtype, name=name, tag=tag or name, align_bytes=64)
+            return sbuf.tile(shape, dtype, name=name, tag=tag or name, align_bytes=64)
 
         def load_list(name, src):
             tile = lists.tile(list(src.shape), U16, name=name)
@@ -48,8 +50,8 @@ def tile_picked_atzmhhaarpagew_none_p_kernel(
             nc.sync.dma_start(tile[:], src[0].rearrange("p n t -> p (n t)").bitcast(I32))
             return tile
 
-        def half(lst, h):
-            return lst[:, h * HALF // 16 : (h + 1) * HALF // 16]
+        def half(entries, which):
+            return entries[:, which * HALF // 16 : (which + 1) * HALF // 16]
 
         def gather_bytes(dst, table, offsets):
             nc.vector.tensor_copy(dst, table[:].indirect(offsets))
@@ -77,196 +79,180 @@ def tile_picked_atzmhhaarpagew_none_p_kernel(
                 stop=stop,
             )
 
-        x_sc = load_scales("x_sc", x_scales, T)
-        l_offs = load_list("l_offs", offs)
-        d_sc = load_scales("d_sc", d_scales, G)
-        l_ka = load_list("l_ka", ka)
-        l_kb = load_list("l_kb", kb)
-        l_n1 = load_list("l_n1", n1)
-        l_n2 = load_list("l_n2", n2)
-        d_w = load_words("d_w", d_words, G)
-        l_k1 = load_list("l_k1", k1)
-        l_k2 = load_list("l_k2", k2)
-        l_hz = load_list("l_hz", hz)
-        l_n5 = load_list("l_n5", n5)
-        x_w = load_words("x_w", x_words, T)
-        l_n6 = load_list("l_n6", n6)
-        l_n3 = load_list("l_n3", n3)
-        l_n4 = load_list("l_n4", n4)
+        x_byte_table = load_scales("x_byte_table", x_scales, T)
+        offs_list = load_list("offs_list", offs)
+        d_byte_table = load_scales("d_byte_table", d_scales, G)
+        ka_list = load_list("ka_list", ka)
+        kb_list = load_list("kb_list", kb)
+        pair_lists = (load_list("n1_list", n1), load_list("n2_list", n2))
+        d_word_table = load_words("d_word_table", d_words, G)
+        k1_list = load_list("k1_list", k1)
+        k2_list = load_list("k2_list", k2)
+        hz_list = load_list("hz_list", hz)
+        n5_list = load_list("n5_list", n5)
+        x_word_table = load_words("x_word_table", x_words, T)
+        n6_list = load_list("n6_list", n6)
+        n3_list = load_list("n3_list", n3)
+        n4_list = load_list("n4_list", n4)
 
-        placed1 = cleared("placed1", 2 * H + S)
-        placed2 = cleared("placed2", 2 * HALF + S)
-        placed3 = cleared("placed3", 2 * HALF)
+        first_placed = cleared("first_placed", 2 * H + S)
+        low_placed = cleared("low_placed", 2 * HALF + S)
+        high_placed = cleared("high_placed", 2 * HALF)
         h2 = [new("h2_%d" % u, [P, S + SPARE], F32) for u in range(4)]
         st = [new("st_%d" % u, [P, S + SPARE], F32) for u in range(4)]
         for u in range(4):
             nc.vector.memset(h2[u][:, S:], 0.0)
             nc.scalar.activation(st[u][:, S:], h2[u][:, S:], COPY)
 
-        bytes1 = new("bytes1", [P, 2 * H + S], U8, tag="hold_a")
-        gather_bytes(bytes1[:, 2 * H :], x_sc, l_offs[:])
-        gather_bytes(bytes1[:, 0:H], d_sc, l_ka[:])
-        gather_bytes(bytes1[:, H : 2 * H], d_sc, l_kb[:])
-        place_rows(placed1, bytes1)
-        xq_scale = placed1[:, 2 * H :]
+        first_bytes = new("first_bytes", [P, 2 * H + S], U8, tag="bytes_and_later_words")
+        gather_bytes(first_bytes[:, 2 * H :], x_byte_table, offs_list[:])
+        gather_bytes(first_bytes[:, 0:H], d_byte_table, ka_list[:])
+        gather_bytes(first_bytes[:, H : 2 * H], d_byte_table, kb_list[:])
+        place_rows(first_placed, first_bytes)
+        xq_scales = first_placed[:, 2 * H :]
+        scales_by_block = first_placed[:, 0 : 2 * H].rearrange("p (l m t) -> p t l m", l=2, t=4)
 
-        def first_product(b, words_a, words_b, scale_a, scale_b):
-            acc = psum.tile([P, 512], F32, name="acc1_%d" % b)
-            product(acc[:, 0:S], words_a, scale_a, xq[:], xq_scale, True, False)
-            product(acc[:, 0:S], words_b, scale_b, xq[:], xq_scale, False, True)
-            h = new("h_%d" % b, [P, S], F32)
-            if b == 0:
-                nc.scalar.activation(h[:], acc[:, 0:S], COPY, scale=0.0625)
-            else:
-                nc.vector.tensor_scalar_mul(h[:], acc[:, 0:S], 0.0625)
+        picked_words = new("picked_words", [P, 2, H], U32)
+        gather_words(picked_words[:, 0, :], d_word_table, ka_list[:])
+        gather_words(picked_words[:, 1, :], d_word_table, kb_list[:])
+        words_by_entry = picked_words[:].rearrange("p l (m t) -> p l m t", t=4)
+        xq_words = new("xq_words", [P, S], U32)
+        gather_words(xq_words[:], x_word_table, offs_list[:])
+
+        def first_sums(t, words, scales):
+            acc = psum.tile([P, BANK], F32, name="first_acc_%d" % t)
+            product(acc[:, 0:S], words[:, 0, :], scales[:, 0, :], xq_words[:], xq_scales, True, False)
+            product(acc[:, 0:S], words[:, 1, :], scales[:, 1, :], xq_words[:], xq_scales, False, True)
+            return acc
+
+        def first_block(t, acc):
+            h = new("h_%d" % t, [P, S], F32)
+            nc.vector.tensor_scalar_mul(h[:], acc[:, 0:S], SIXTEENTH)
             return h
 
-        def combine(b, pairs, tag):
-            total = new("total_%d" % b, [P, W], F32, tag=tag)
-            rb = new("rb_%d" % b, [P, W], F32)
-            nc.vector.tensor_tensor(total[:], pairs[0], pairs[1], ALU.add)
-            nc.vector.tensor_tensor(rb[:], pairs[0], pairs[1], ALU.subtract)
+        def fetch_pairs(t, h):
+            pairs = new("pairs_%d" % t, [P, 2, W], F32)
+            for side in range(2):
+                nc.scalar.activation(pairs[:, side, :], h[:].indirect(pair_lists[side][:]), COPY)
+            return pairs
+
+        def sum_and_difference(t, pairs):
+            total = new("total_%d" % t, [P, W], F32)
+            rb = new("rb_%d" % t, [P, W], F32)
+            nc.vector.tensor_tensor(total[:], pairs[:, 0, :], pairs[:, 1, :], ALU.add)
+            nc.vector.tensor_tensor(rb[:], pairs[:, 0, :], pairs[:, 1, :], ALU.subtract)
             return total, rb
 
-        def fetch(pairs, h, side):
-            nc.scalar.activation(pairs[side], h[:].indirect((l_n1, l_n2)[side][:]), COPY)
+        def put_back(blocks, values):
+            for side, factor in enumerate((0.75, 1.0)):
+                for t, both in zip(blocks, values):
+                    nc.scalar.activation(ub[t][:].indirect(pair_lists[side][:]), both[side][:], COPY, scale=factor)
 
-        def put(ub, both, side):
-            nc.scalar.activation(ub[:].indirect((l_n1, l_n2)[side][:]), both[side][:], COPY, scale=(0.75, 1.0)[side])
-
-        placed_rows = placed1[:, 0 : 2 * H].rearrange("p (l m t) -> p t l m", l=2, t=4)
-        words1 = new("words1", [P, 2, H], U32)
-        gather_words(words1[:, 0, :], d_w, l_ka[:])
-        gather_words(words1[:, 1, :], d_w, l_kb[:])
-        word_rows = words1[:].rearrange("p l (m t) -> p l m t", t=4)
-        xq = new("xq", [P, S], U32)
-        gather_words(xq[:], x_w, l_offs[:])
-        first_words = new("first_words", [P, 2, P], U32, tag="hold_g")
-        nc.vector.tensor_copy(first_words[:], word_rows[:, :, :, 0])
-        first_scales = new("first_scales", [P, 2, P], U8)
-        nc.vector.tensor_copy(first_scales[:], placed_rows[:, 0])
-        h = [first_product(0, first_words[:, 0, :], first_words[:, 1, :], first_scales[:, 0, :], first_scales[:, 1, :])]
-        gains = new("gains", [P, 4], F32, tag="hold_g")
+        words_0 = new("words_0", [P, 2, P], U32, tag="words_0_and_later_scales")
+        nc.vector.tensor_copy(words_0[:], words_by_entry[:, :, :, 0])
+        scales_0 = new("scales_0", [P, 2, P], U8, tag="scales_0_and_gains")
+        nc.vector.tensor_copy(scales_0[:], scales_by_block[:, 0])
+        acc_0 = first_sums(0, words_0, scales_0)
+        words_123 = new("words_123", [P, 3, 2, P], U32, tag="bytes_and_later_words")
+        nc.vector.tensor_copy(words_123[:].rearrange("p t l m -> p l m t"), words_by_entry[:, :, :, 1:4])
+        scales_1 = new("scales_1", [P, 2, P], U8)
+        nc.vector.tensor_copy(scales_1[:], scales_by_block[:, 1])
+        h_0 = first_block(0, acc_0)
+        scales_23 = new("scales_23", [P, 2, 2, P], U8, tag="words_0_and_later_scales")
+        nc.vector.tensor_copy(scales_23[:], scales_by_block[:, 2:4])
+        gains = new("gains", [P, 4], F32, tag="scales_0_and_gains")
         nc.sync.dma_start(gains[:], gs.rearrange("(p t) o -> p (t o)", t=4))
 
-        rest_words = new("rest_words", [P, 3, 2, P], U32, tag="hold_a")
-        nc.vector.tensor_copy(rest_words[:].rearrange("p t l m -> p l m t"), word_rows[:, :, :, 1:4])
-        rest_scales = new("rest_scales", [P, 3, 2, P], U8, tag="hold_s")
-        nc.vector.tensor_copy(rest_scales[:, 0], placed_rows[:, 1])
-        nc.vector.tensor_copy(rest_scales[:, 1:3], placed_rows[:, 2:4])
-
-        def rest_product(t):
-            words, scales = rest_words[:, t - 1], rest_scales[:, t - 1]
-            return first_product(t, words[:, 0, :], words[:, 1, :], scales[:, 0, :], scales[:, 1, :])
-
         ub = [new("ub_%d" % t, [P, S], F32) for t in range(4)]
-        pair_tiles = [new("pairs_%d" % t, [P, 2, W], F32) for t in range(4)]
-        pairs = [[tile[:, 0, :], tile[:, 1, :]] for tile in pair_tiles]
-        h.append(rest_product(1))
-        for t in (0, 1):
-            fetch(pairs[t], h[t], 0)
-            fetch(pairs[t], h[t], 1)
-        h.append(rest_product(2))
-        both_a = combine(0, pairs[0], None)
-        h.append(rest_product(3))
-        both_b = combine(1, pairs[1], None)
-        for side in range(2):
-            put(ub[0], both_a, side)
-            put(ub[1], both_b, side)
-        for t in (2, 3):
-            fetch(pairs[t], h[t], 0)
-            fetch(pairs[t], h[t], 1)
+        h_1 = first_block(1, first_sums(1, words_123[:, 0], scales_1))
+        pairs_0 = fetch_pairs(0, h_0)
+        pairs_1 = fetch_pairs(1, h_1)
+        values_0 = sum_and_difference(0, pairs_0)
+        h_2 = first_block(2, first_sums(2, words_123[:, 1], scales_23[:, 0]))
+        values_1 = sum_and_difference(1, pairs_1)
+        h_3 = first_block(3, first_sums(3, words_123[:, 2], scales_23[:, 1]))
+        put_back((0, 1), (values_0, values_1))
+        pairs_2 = fetch_pairs(2, h_2)
+        pairs_3 = fetch_pairs(3, h_3)
 
-        bytes2 = new("bytes2", [P, 2 * HALF + S], U8, tag="hold_a")
-        gather_bytes(bytes2[:, 0:HALF], d_sc, half(l_k1, 0))
-        gather_bytes(bytes2[:, HALF : 2 * HALF], d_sc, half(l_k2, 0))
-        gather_bytes(bytes2[:, 2 * HALF :], x_sc, l_hz[:])
-        place_rows(placed2, bytes2)
-        words2 = new("words2", [P, 3, HALF], U32, tag="hold_s")
-        gather_words(words2[:, 1, :], d_w, half(l_k2, 0))
-        gather_words(words2[:, 2, :], x_w, l_hz[:])
-        both_c = combine(2, pairs[2], None)
-        both_d = combine(3, pairs[3], None)
-        gather_words(words2[:, 0, :], d_w, half(l_k1, 0))
-        xh, xh_scale = words2[:, 2, :], placed2[:, 2 * HALF :]
-        words2 = (words2[:, 0, :], words2[:, 1, :])
-        for side in range(2):
-            put(ub[2], both_c, side)
-            put(ub[3], both_d, side)
+        low_bytes = new("low_bytes", [P, 2 * HALF + S], U8, tag="bytes_and_later_words")
+        gather_bytes(low_bytes[:, 0:HALF], d_byte_table, half(k1_list, 0))
+        gather_bytes(low_bytes[:, HALF : 2 * HALF], d_byte_table, half(k2_list, 0))
+        gather_bytes(low_bytes[:, 2 * HALF :], x_byte_table, hz_list[:])
+        place_rows(low_placed, low_bytes)
+        low_words = new("low_words", [P, 3, HALF], U32, tag="words_0_and_later_scales")
+        gather_words(low_words[:, 1, :], d_word_table, half(k2_list, 0))
+        gather_words(low_words[:, 2, :], x_word_table, hz_list[:])
+        values_2 = sum_and_difference(2, pairs_2)
+        values_3 = sum_and_difference(3, pairs_3)
+        gather_words(low_words[:, 0, :], d_word_table, half(k1_list, 0))
+        xh_words, xh_scales = low_words[:, 2, :], low_placed[:, 2 * HALF :]
+        put_back((2, 3), (values_2, values_3))
 
-        halves = (slice(0, P), slice(P, S))
+        column_halves = (slice(0, P), slice(P, S))
         z = [new("z_%d" % c, [P, P, 4], BF16) for c in range(2)]
-
-        def weave(t, plane, gain):
-            for c in range(2):
-                nc.vector.tensor_scalar_mul(z[c][:, :, t], plane[:, halves[c]], gain)
-
         for t in range(4):
-            weave(t, ub[t], gains[:, t : t + 1])
+            for c in range(2):
+                nc.vector.tensor_scalar_mul(z[c][:, :, t], ub[t][:, column_halves[c]], gains[:, t : t + 1])
         z_words = new("z_words", [P, S], U32)
-        z_scale = new("z_scale", [P, S], U8)
+        z_scales = new("z_scales", [P, S], U8)
         for c in range(2):
             nc.vector.quantize_mx(
-                out=z_words[:, halves[c]].bitcast(FP8X4),
-                scales=z_scale[:, halves[c]],
+                out=z_words[:, column_halves[c]].bitcast(FP8X4),
+                scales=z_scales[:, column_halves[c]],
                 in_=z[c][:].rearrange("p n t -> p (n t)"),
             )
 
-        def second_product(u, words, placed):
-            cols = slice(P * (u % 2), P * (u % 2) + P)
-            acc = psum.tile([P, 512], F32, name="acc2_%d" % u)
-            product(acc[:, 0:S], words[1][:, cols], placed[:, HALF : 2 * HALF][:, cols], xh, xh_scale, True, False)
-            pieces = halves if u == 0 else (slice(0, S),)
+        def second_block(u, words, placed, pieces):
+            rows = slice(P * (u % 2), P * (u % 2) + P)
+            k1_words, k1_scales = words[:, 0, rows], placed[:, 0:HALF][:, rows]
+            k2_words, k2_scales = words[:, 1, rows], placed[:, HALF : 2 * HALF][:, rows]
+            acc = psum.tile([P, BANK], F32, name="second_acc_%d" % u)
+            product(acc[:, 0:S], k2_words, k2_scales, xh_words, xh_scales, True, False)
             for piece in pieces:
-                product(
-                    acc[:, piece],
-                    words[0][:, cols],
-                    placed[:, 0:HALF][:, cols],
-                    z_words[:, piece],
-                    z_scale[:, piece],
-                    False,
-                    piece.stop == S,
-                )
-            nc.vector.tensor_scalar_mul(h2[u][:, 0:S], acc[:, 0:S], 0.0625)
+                last = piece.stop == S
+                product(acc[:, piece], k1_words, k1_scales, z_words[:, piece], z_scales[:, piece], False, last)
+            nc.vector.tensor_scalar_mul(h2[u][:, 0:S], acc[:, 0:S], SIXTEENTH)
 
-        def step(u):
-            other = new("other_%d" % u, [P, S], F32, tag="hold_d" if u == 0 else None)
-            nc.scalar.activation(other[:], h2[u][:].indirect(l_n5[:]), COPY)
+        def step(u, tag=None):
+            other = new("other_%d" % u, [P, S], F32, tag=tag)
+            nc.scalar.activation(other[:], h2[u][:].indirect(n5_list[:]), COPY)
             nc.vector.tensor_tensor(st[u][:, 0:S], h2[u][:, 0:S], other[:], ALU.subtract)
 
-        def rival_and_first_put(u):
-            rival = new("rival_%d" % u, [P, S], F32, tag="hold_e" if u == 0 else None)
+        def larger_and_first_put(u, tag=None):
+            rival = new("rival_%d" % u, [P, S], F32, tag=tag)
             up = new("up_%d" % u, [P, S], F32)
             page = new("page_%d" % u, [P, U], F32)
-            nc.scalar.activation(rival[:], st[u][:].indirect(l_n6[:]), COPY)
+            nc.scalar.activation(rival[:], st[u][:].indirect(n6_list[:]), COPY)
             nc.vector.tensor_tensor(up[:], st[u][:, 0:S], rival[:], ALU.max)
-            nc.scalar.activation(page[:].indirect(l_n3[:]), st[u][:, 0:S], COPY)
+            nc.scalar.activation(page[:].indirect(n3_list[:]), st[u][:, 0:S], COPY)
             return up, page
 
-        def second_put(u, up, page):
-            nc.scalar.activation(page[:].indirect(l_n4[:]), up[:], COPY)
+        def second_put_and_store(u, up, page):
+            nc.scalar.activation(page[:].indirect(n4_list[:]), up[:], COPY)
             nc.sync.dma_start(out[P * u : P * u + P, :], page[:])
 
-        second_product(0, words2, placed2)
-        second_product(1, words2, placed2)
-        step(0)
-        bytes3 = new("bytes3", [P, 2 * HALF], U8, tag="hold_d")
-        gather_bytes(bytes3[:, 0:HALF], d_sc, half(l_k1, 1))
-        gather_bytes(bytes3[:, HALF:], d_sc, half(l_k2, 1))
-        place_rows(placed3, bytes3)
+        all_columns = (slice(0, S),)
+        second_block(0, low_words, low_placed, column_halves)
+        second_block(1, low_words, low_placed, all_columns)
+        step(0, tag="other_0_and_high_bytes")
+        high_bytes = new("high_bytes", [P, 2 * HALF], U8, tag="other_0_and_high_bytes")
+        gather_bytes(high_bytes[:, 0:HALF], d_byte_table, half(k1_list, 1))
+        gather_bytes(high_bytes[:, HALF:], d_byte_table, half(k2_list, 1))
+        place_rows(high_placed, high_bytes)
         step(1)
-        first = rival_and_first_put(0)
-        words3 = new("words3", [P, 2, HALF], U32, tag="hold_e")
-        gather_words(words3[:, 1, :], d_w, half(l_k2, 1))
-        gather_words(words3[:, 0, :], d_w, half(l_k1, 1))
-        second = rival_and_first_put(1)
-        second_put(0, *first)
-        second_put(1, *second)
+        begun_0 = larger_and_first_put(0, tag="rival_0_and_high_words")
+        high_words = new("high_words", [P, 2, HALF], U32, tag="rival_0_and_high_words")
+        gather_words(high_words[:, 1, :], d_word_table, half(k2_list, 1))
+        gather_words(high_words[:, 0, :], d_word_table, half(k1_list, 1))
+        begun_1 = larger_and_first_put(1)
+        second_put_and_store(0, *begun_0)
+        second_put_and_store(1, *begun_1)
         for u in (2, 3):
-            second_product(u, (words3[:, 0, :], words3[:, 1, :]), placed3)
+            second_block(u, high_words, high_placed, all_columns)
         for u in (2, 3):
             step(u)
-        first = rival_and_first_put(2)
-        second = rival_and_first_put(3)
-        second_put(2, *first)
-        second_put(3, *second)
+        begun_2 = larger_and_first_put(2)
+        begun_3 = larger_and_first_put(3)
+        second_put_and_store(2, *begun_2)
+        second_put_and_store(3, *begun_3)

from contextlib import ExitStack

import concourse.mybir as mybir

K, T, S, G, H, W, U = 512, 1024, 256, 2048, 512, 128, 512
FLOPS = 4 * 2 * K * H * S

F32 = mybir.dt.float32
BF16 = mybir.dt.bfloat16
I32 = mybir.dt.int32
U32 = mybir.dt.uint32
U16 = mybir.dt.uint16
U8 = mybir.dt.uint8
FP8X4 = mybir.dt.float8_e4m3fn_x4
COPY = mybir.ActivationFunctionType.Copy
ALU = mybir.AluOpType

P = 128
BANK = 512
HALF = H // 2
SPARE = 16
SIXTEENTH = 0.0625


def tile_picked_atzmhhaarpagew_none_p_kernel(
    tc, x_words, x_scales, d_words, d_scales, gs, offs, ka, kb, n1, n2, k1, k2, hz, n3, n4, n5, n6, out
):
    nc = tc.nc
    with ExitStack() as ctx:
        lists = ctx.enter_context(tc.tile_pool(name="lists", bufs=1))
        sbuf = ctx.enter_context(tc.tile_pool(name="sbuf", bufs=1))
        psum = ctx.enter_context(tc.psum_pool(name="psum", bufs=1))

        def new(name, shape, dtype, tag=None):
            return sbuf.tile(shape, dtype, name=name, tag=tag or name, align_bytes=64)

        def load_list(name, src):
            tile = lists.tile(list(src.shape), U16, name=name)
            nc.sync.dma_start(tile[:], src)
            return tile

        def load_scales(name, src, width):
            tile = new(name, [P, width], U8)
            rows = src[0].bitcast(I32).unsqueeze(1).broadcast_to([16, 8, width // 4])
            nc.sync.dma_start(tile[:].bitcast(I32), rows)
            return tile

        def load_words(name, src, width):
            tile = new(name, [P, width], I32)
            nc.sync.dma_start(tile[:], src[0].rearrange("p n t -> p (n t)").bitcast(I32))
            return tile

        def half(entries, which):
            return entries[:, which * HALF // 16 : (which + 1) * HALF // 16]

        def gather_bytes(dst, table, offsets):
            nc.vector.tensor_copy(dst, table[:].indirect(offsets))

        def gather_words(dst, table, offsets):
            nc.vector.tensor_copy(dst, table[:].bitcast(U32).indirect(offsets))

        def cleared(name, width):
            tile = new(name, [P, width], U8)
            nc.vector.memset(tile[:].bitcast(I32), 0)
            return tile

        def place_rows(dst, src):
            for r in range(4):
                nc.sync.dma_start(dst[r:P:32, :].bitcast(I32), src[8 * r : P : 32, :].bitcast(I32))

        def product(acc, lhs, lhs_scale, rhs, rhs_scale, start, stop):
            nc.tensor.matmul_mx(
                out=acc,
                lhsT=lhs.bitcast(FP8X4),
                lhsT_scale=lhs_scale,
                rhs=rhs.bitcast(FP8X4),
                rhs_scale=rhs_scale,
                start=start,
                stop=stop,
            )

        x_byte_table = load_scales("x_byte_table", x_scales, T)
        offs_list = load_list("offs_list", offs)
        d_byte_table = load_scales("d_byte_table", d_scales, G)
        ka_list = load_list("ka_list", ka)
        kb_list = load_list("kb_list", kb)
        pair_lists = (load_list("n1_list", n1), load_list("n2_list", n2))
        d_word_table = load_words("d_word_table", d_words, G)
        k1_list = load_list("k1_list", k1)
        k2_list = load_list("k2_list", k2)
        hz_list = load_list("hz_list", hz)
        n5_list = load_list("n5_list", n5)
        x_word_table = load_words("x_word_table", x_words, T)
        n6_list = load_list("n6_list", n6)
        n3_list = load_list("n3_list", n3)
        n4_list = load_list("n4_list", n4)

        first_placed = cleared("first_placed", 2 * H + S)
        low_placed = cleared("low_placed", 2 * HALF + S)
        high_placed = cleared("high_placed", 2 * HALF)
        h2 = [new("h2_%d" % u, [P, S + SPARE], F32) for u in range(4)]
        st = [new("st_%d" % u, [P, S + SPARE], F32) for u in range(4)]
        for u in range(4):
            nc.vector.memset(h2[u][:, S:], 0.0)
            nc.scalar.activation(st[u][:, S:], h2[u][:, S:], COPY)

        first_bytes = new("first_bytes", [P, 2 * H + S], U8, tag="bytes_and_later_words")
        gather_bytes(first_bytes[:, 2 * H :], x_byte_table, offs_list[:])
        gather_bytes(first_bytes[:, 0:H], d_byte_table, ka_list[:])
        gather_bytes(first_bytes[:, H : 2 * H], d_byte_table, kb_list[:])
        place_rows(first_placed, first_bytes)
        xq_scales = first_placed[:, 2 * H :]
        scales_by_block = first_placed[:, 0 : 2 * H].rearrange("p (l m t) -> p t l m", l=2, t=4)

        picked_words = new("picked_words", [P, 2, H], U32)
        gather_words(picked_words[:, 0, :], d_word_table, ka_list[:])
        gather_words(picked_words[:, 1, :], d_word_table, kb_list[:])
        words_by_entry = picked_words[:].rearrange("p l (m t) -> p l m t", t=4)
        xq_words = new("xq_words", [P, S], U32)
        gather_words(xq_words[:], x_word_table, offs_list[:])

        def first_sums(t, words, scales):
            acc = psum.tile([P, BANK], F32, name="first_acc_%d" % t)
            product(acc[:, 0:S], words[:, 0, :], scales[:, 0, :], xq_words[:], xq_scales, True, False)
            product(acc[:, 0:S], words[:, 1, :], scales[:, 1, :], xq_words[:], xq_scales, False, True)
            return acc

        def first_block(t, acc):
            h = new("h_%d" % t, [P, S], F32)
            nc.vector.tensor_scalar_mul(h[:], acc[:, 0:S], SIXTEENTH)
            return h

        def fetch_pairs(t, h):
            pairs = new("pairs_%d" % t, [P, 2, W], F32)
            for side in range(2):
                nc.scalar.activation(pairs[:, side, :], h[:].indirect(pair_lists[side][:]), COPY)
            return pairs

        def sum_and_difference(t, pairs):
            total = new("total_%d" % t, [P, W], F32)
            rb = new("rb_%d" % t, [P, W], F32)
            nc.vector.tensor_tensor(total[:], pairs[:, 0, :], pairs[:, 1, :], ALU.add)
            nc.vector.tensor_tensor(rb[:], pairs[:, 0, :], pairs[:, 1, :], ALU.subtract)
            return total, rb

        def put_back(blocks, values):
            for side, factor in enumerate((0.75, 1.0)):
                for t, both in zip(blocks, values):
                    nc.scalar.activation(ub[t][:].indirect(pair_lists[side][:]), both[side][:], COPY, scale=factor)

        words_0 = new("words_0", [P, 2, P], U32, tag="words_0_and_later_scales")
        nc.vector.tensor_copy(words_0[:], words_by_entry[:, :, :, 0])
        scales_0 = new("scales_0", [P, 2, P], U8, tag="scales_0_and_gains")
        nc.vector.tensor_copy(scales_0[:], scales_by_block[:, 0])
        acc_0 = first_sums(0, words_0, scales_0)
        words_123 = new("words_123", [P, 3, 2, P], U32, tag="bytes_and_later_words")
        nc.vector.tensor_copy(words_123[:].rearrange("p t l m -> p l m t"), words_by_entry[:, :, :, 1:4])
        scales_1 = new("scales_1", [P, 2, P], U8)
        nc.vector.tensor_copy(scales_1[:], scales_by_block[:, 1])
        h_0 = first_block(0, acc_0)
        scales_23 = new("scales_23", [P, 2, 2, P], U8, tag="words_0_and_later_scales")
        nc.vector.tensor_copy(scales_23[:], scales_by_block[:, 2:4])
        gains = new("gains", [P, 4], F32, tag="scales_0_and_gains")
        nc.sync.dma_start(gains[:], gs.rearrange("(p t) o -> p (t o)", t=4))

        ub = [new("ub_%d" % t, [P, S], F32) for t in range(4)]
        h_1 = first_block(1, first_sums(1, words_123[:, 0], scales_1))
        pairs_0 = fetch_pairs(0, h_0)
        pairs_1 = fetch_pairs(1, h_1)
        values_0 = sum_and_difference(0, pairs_0)
        h_2 = first_block(2, first_sums(2, words_123[:, 1], scales_23[:, 0]))
        values_1 = sum_and_difference(1, pairs_1)
        h_3 = first_block(3, first_sums(3, words_123[:, 2], scales_23[:, 1]))
        put_back((0, 1), (values_0, values_1))
        pairs_2 = fetch_pairs(2, h_2)
        pairs_3 = fetch_pairs(3, h_3)

        low_bytes = new("low_bytes", [P, 2 * HALF + S], U8, tag="bytes_and_later_words")
        gather_bytes(low_bytes[:, 0:HALF], d_byte_table, half(k1_list, 0))
        gather_bytes(low_bytes[:, HALF : 2 * HALF], d_byte_table, half(k2_list, 0))
        gather_bytes(low_bytes[:, 2 * HALF :], x_byte_table, hz_list[:])
        place_rows(low_placed, low_bytes)
        low_words = new("low_words", [P, 3, HALF], U32, tag="words_0_and_later_scales")
        gather_words(low_words[:, 1, :], d_word_table, half(k2_list, 0))
        gather_words(low_words[:, 2, :], x_word_table, hz_list[:])
        values_2 = sum_and_difference(2, pairs_2)
        values_3 = sum_and_difference(3, pairs_3)
        gather_words(low_words[:, 0, :], d_word_table, half(k1_list, 0))
        xh_words, xh_scales = low_words[:, 2, :], low_placed[:, 2 * HALF :]
        put_back((2, 3), (values_2, values_3))

        column_halves = (slice(0, P), slice(P, S))
        z = [new("z_%d" % c, [P, P, 4], BF16) for c in range(2)]
        for t in range(4):
            for c in range(2):
                nc.vector.tensor_scalar_mul(z[c][:, :, t], ub[t][:, column_halves[c]], gains[:, t : t + 1])
        z_words = new("z_words", [P, S], U32)
        z_scales = new("z_scales", [P, S], U8)
        for c in range(2):
            nc.vector.quantize_mx(
                out=z_words[:, column_halves[c]].bitcast(FP8X4),
                scales=z_scales[:, column_halves[c]],
                in_=z[c][:].rearrange("p n t -> p (n t)"),
            )

        def second_block(u, words, placed, pieces):
            rows = slice(P * (u % 2), P * (u % 2) + P)
            k1_words, k1_scales = words[:, 0, rows], placed[:, 0:HALF][:, rows]
            k2_words, k2_scales = words[:, 1, rows], placed[:, HALF : 2 * HALF][:, rows]
            acc = psum.tile([P, BANK], F32, name="second_acc_%d" % u)
            product(acc[:, 0:S], k2_words, k2_scales, xh_words, xh_scales, True, False)
            for piece in pieces:
                last = piece.stop == S
                product(acc[:, piece], k1_words, k1_scales, z_words[:, piece], z_scales[:, piece], False, last)
            nc.vector.tensor_scalar_mul(h2[u][:, 0:S], acc[:, 0:S], SIXTEENTH)

        def step(u, tag=None):
            other = new("other_%d" % u, [P, S], F32, tag=tag)
            nc.scalar.activation(other[:], h2[u][:].indirect(n5_list[:]), COPY)
            nc.vector.tensor_tensor(st[u][:, 0:S], h2[u][:, 0:S], other[:], ALU.subtract)

        def larger_and_first_put(u, tag=None):
            rival = new("rival_%d" % u, [P, S], F32, tag=tag)
            up = new("up_%d" % u, [P, S], F32)
            page = new("page_%d" % u, [P, U], F32)
            nc.scalar.activation(rival[:], st[u][:].indirect(n6_list[:]), COPY)
            nc.vector.tensor_tensor(up[:], st[u][:, 0:S], rival[:], ALU.max)
            nc.scalar.activation(page[:].indirect(n3_list[:]), st[u][:, 0:S], COPY)
            return up, page

        def second_put_and_store(u, up, page):
            nc.scalar.activation(page[:].indirect(n4_list[:]), up[:], COPY)
            nc.sync.dma_start(out[P * u : P * u + P, :], page[:])

        all_columns = (slice(0, S),)
        second_block(0, low_words, low_placed, column_halves)
        second_block(1, low_words, low_placed, all_columns)
        step(0, tag="other_0_and_high_bytes")
        high_bytes = new("high_bytes", [P, 2 * HALF], U8, tag="other_0_and_high_bytes")
        gather_bytes(high_bytes[:, 0:HALF], d_byte_table, half(k1_list, 1))
        gather_bytes(high_bytes[:, HALF:], d_byte_table, half(k2_list, 1))
        place_rows(high_placed, high_bytes)
        step(1)
        begun_0 = larger_and_first_put(0, tag="rival_0_and_high_words")
        high_words = new("high_words", [P, 2, HALF], U32, tag="rival_0_and_high_words")
        gather_words(high_words[:, 1, :], d_word_table, half(k2_list, 1))
        gather_words(high_words[:, 0, :], d_word_table, half(k1_list, 1))
        begun_1 = larger_and_first_put(1)
        second_put_and_store(0, *begun_0)
        second_put_and_store(1, *begun_1)
        for u in (2, 3):
            second_block(u, high_words, high_placed, all_columns)
        for u in (2, 3):
            step(u)
        begun_2 = larger_and_first_put(2)
        begun_3 = larger_and_first_put(3)
        second_put_and_store(2, *begun_2)
        second_put_and_store(3, *begun_3)
